import numpy as np, ml_dtypes
CORES = [3,11,19,27,35,43,131,139,147,155,163,171]
N = 12
KT, F = 2, 128
def setup_inputs(rng):
    return {"a": rng.standard_normal((N, 128, KT * 128), dtype=np.float32).astype(ml_dtypes.bfloat16), "w": rng.standard_normal((N, 128, KT * F), dtype=np.float32).astype(ml_dtypes.bfloat16)}
def reference(a, w):
    A, W = a.astype(np.float64), w.astype(np.float64)
    y = np.zeros((N, 128, N * F))
    for r in range(N):
        for j in range(N):
            for t in range(KT):
                y[r][:, F * j:F * j + F] += A[j][:, 128 * t:128 * t + 128].T @ W[r][:, F * t:F * t + F]
    return {"y": y.astype(ml_dtypes.bfloat16 if a.dtype != np.float64 else np.float64)}

@@ -1,0 +1,112 @@
+from concourse.bass import DstId, RemoteDMATransfer
+
+N = 12
+RANK_CORE = 3
+
+SCRATCH = {
+    "ad": ("dram", [128, 256], "bfloat16"),
+    "ag": ("sbuf", [128, N * 256], "bfloat16"),
+    "ws": ("sbuf", [128, 256], "bfloat16"),
+    "ys": ("sbuf", [128, N * 128], "bfloat16"),
+}
+for _i in range(6):
+    SCRATCH["ps%d" % _i] = ("psum", [128, 512], "float32")
+
+SEMAPHORES = (["ld_ad", "ld", "fan", "snt", "aR", "aF", "aS", "st_a", "st_b"]
+              + ["mm%d" % i for i in range(6)] + ["cp%d" % i for i in range(6)])
+
+DIRECT = [(0, 0, 1), (0, 1, 0), (0, 1, 1), (0, 2, 0)]
+HELP = {
+    2: [(0, 2, 1), (1, 0, 0)],
+    4: [(1, 1, 0), (1, 2, 0)],
+    6: [(1, 1, 1), (1, 2, 1)],
+    7: [(1, 0, 1)],
+}
+FAN_ORDER = [2, 4, 6, 7]
+
+
+def _to(r, d):
+    return 6 * ((r // 6) ^ d[0]) + 2 * (((r % 6) // 2 + d[1]) % 3) + ((r % 2) ^ d[2])
+
+
+def _from(r, d):
+    return 6 * ((r // 6) ^ d[0]) + 2 * (((r % 6) // 2 - d[1]) % 3) + ((r % 2) ^ d[2])
+
+
+def _helper(g, core, T, topo, rank):
+    slot = T.ag[:, 256 * rank:256 * rank + 256]
+    g.wait_ge(T.sem.fan, 8)
+    sems = [T.sem.aF, T.sem.aS]
+    plan = HELP[core % 8]
+    for k, d in enumerate(plan):
+        dst = T.cores[_to(rank, d)]
+        rid, pid = topo.addr(dst, core)
+        g.remote_dma(slot, T.ad[:, :], sems[k], T.sem.snt, pid, rid, 0x00FF)
+    g.wait_ge(T.sem.snt, 8 * len(plan))
+
+
+def rank_program(g, core, T, topo):
+    rank = T.rank_of(core)
+    if rank is None:
+        home = core - core % 8 + RANK_CORE
+        r = T.rank_of(home)
+        if r is not None and core % 8 in HELP:
+            _helper(g, core, T, topo, r)
+        return
+
+    own = T.ag[:, 256 * rank:256 * rank + 256]
+    g.sync.dma_start(T.ad[:, :], T.a[:, :]).then_inc(T.sem.ld_ad, 16)
+    g.sync.dma_start(T.ws[:, :], T.w[:, :]).then_inc(T.sem.ld, 16)
+    g.sync.dma_start(own, T.a[:, :]).then_inc(T.sem.ld, 16)
+
+    def ids(cs):
+        out = []
+        for c in cs:
+            rid, pid = topo.addr(c, core)
+            out.append(DstId(rid=rid, pnc=pid))
+        return out
+    helpers = [core - RANK_CORE + h for h in FAN_ORDER]
+    direct = [T.cores[_to(rank, d)] for d in DIRECT]
+    g.wait_ge(T.sem.ld_ad, 16)
+    g.remote_dma_fused([
+        RemoteDMATransfer(dst_ids=ids(helpers), dma_engine_mask=0xFF00, remote_sem=T.sem.fan,
+                          srcs=[T.ad[:, :]], dsts=[T.ad[:, :] for _ in helpers]),
+        RemoteDMATransfer(dst_ids=ids(direct), dma_engine_mask=0x00FF, remote_sem=T.sem.aR,
+                          srcs=[T.ad[:, :]], dsts=[own for _ in direct]),
+    ], local_sem=T.sem.snt)
+
+    stages = [
+        (T.sem.ld, 32, [(0, 0, 0)]),
+        (T.sem.aR, 8 * len(DIRECT), DIRECT),
+        (T.sem.aF, 8 * len(HELP), [HELP[h][0] for h in FAN_ORDER]),
+        (T.sem.aS, 8 * sum(1 for h in HELP if len(HELP[h]) > 1), [HELP[h][1] for h in FAN_ORDER if len(HELP[h]) > 1]),
+    ]
+    done = {}
+    pair_order = []
+    for sem, val, ds in stages:
+        g.tensor.wait_ge(sem, val)
+        js = [_from(rank, d) for d in ds]
+        js.sort(key=lambda j: (0 if done.get(j // 2, 0) else 1, j))
+        for j in js:
+            p = j // 2
+            for t in range(2):
+                g.tensor.matmul(T["ps%d" % p][:, 128 * (j % 2):128 * (j % 2) + 128],
+                                T.ag[:, 256 * j + 128 * t:256 * j + 128 * t + 128],
+                                T.ws[:, 128 * t:128 * t + 128],
+                                t == 0, t == 1).then_inc(T.sem["mm%d" % p], 1)
+            done[p] = done.get(p, 0) + 1
+            if done[p] == 2:
+                pair_order.append(p)
+
+    nst = [0, 0]
+    for i, p in enumerate(pair_order):
+        cols = slice(256 * p, 256 * p + 256)
+        g.vector.wait_ge(T.sem["mm%d" % p], 4)
+        g.vector.tensor_copy(T.ys[:, cols], T["ps%d" % p][:, 0:256]).then_inc(T.sem["cp%d" % p], 1)
+        q, st = ((g.sync, T.sem.st_a), (g.scalar, T.sem.st_b))[i % 2]
+        q.wait_ge(T.sem["cp%d" % p], 1)
+        q.dma_start(T.y[:, cols], T.ys[:, cols]).then_inc(st, 16)
+        nst[i % 2] += 16
+    g.sync.wait_ge(T.sem.st_a, nst[0])
+    g.scalar.wait_ge(T.sem.st_b, nst[1])
+    g.wait_ge(T.sem.snt, 16)

@@ -3,26 +3,32 @@ from concourse.bass import DstId, RemoteDMATransfer
 N = 12
 RANK_CORE = 3
 
+OWN = (0, 0, 0)
+D12 = [(0, 1, 0), (0, 2, 0)]
+D3 = (1, 0, 0)
+FWD = [(0, 1, 1), (0, 2, 1)]
+HELP = {
+    6: [(1, 1, 1), (1, 2, 1)],
+    7: [(0, 0, 1), (1, 2, 0)],
+    2: [(1, 0, 1), (1, 1, 0)],
+}
+FAN_ORDER = [6, 7, 2]
+WAVE1 = [HELP[h][0] for h in FAN_ORDER]
+WAVE2 = [HELP[h][1] for h in FAN_ORDER]
+SLOTS = [OWN] + D12 + FWD + [D3] + WAVE1 + WAVE2
+BANKS = [D12, [OWN, (0, 0, 1)], [(1, 0, 0), (1, 0, 1)], [(1, 1, 0), (1, 1, 1)], [(1, 2, 0), (1, 2, 1)], FWD]
+
 SCRATCH = {
     "ad": ("dram", [128, 256], "bfloat16"),
     "ag": ("sbuf", [128, N * 256], "bfloat16"),
     "ws": ("sbuf", [128, 256], "bfloat16"),
     "ys": ("sbuf", [128, N * 128], "bfloat16"),
 }
-for _i in range(6):
+for _i in range(len(BANKS)):
     SCRATCH["ps%d" % _i] = ("psum", [128, 512], "float32")
 
-SEMAPHORES = (["ld_ad", "ld", "fan", "snt", "aR", "aF", "aS", "st_a", "st_b"]
-              + ["mm%d" % i for i in range(6)] + ["cp%d" % i for i in range(6)])
-
-DIRECT = [(0, 0, 1), (0, 1, 0), (0, 1, 1), (0, 2, 0)]
-HELP = {
-    2: [(0, 2, 1), (1, 0, 0)],
-    4: [(1, 1, 0), (1, 2, 0)],
-    6: [(1, 1, 1), (1, 2, 1)],
-    7: [(1, 0, 1)],
-}
-FAN_ORDER = [2, 4, 6, 7]
+SEMAPHORES = (["ld_ad", "ld", "fan", "snt", "aR", "aD", "aW", "aF", "aS", "st_a", "st_b"]
+              + ["mm%d" % i for i in range(len(BANKS))] + ["cp%d" % i for i in range(len(BANKS))])
 
 
 def _to(r, d):
@@ -33,31 +39,32 @@ def _from(r, d):
     return 6 * ((r // 6) ^ d[0]) + 2 * (((r % 6) // 2 - d[1]) % 3) + ((r % 2) ^ d[2])
 
 
+def _slot(T, d, n=1):
+    s = SLOTS.index(d)
+    return T.ag[:, 256 * s:256 * (s + n)]
+
+
 def _helper(g, core, T, topo, rank):
-    slot = T.ag[:, 256 * rank:256 * rank + 256]
     g.wait_ge(T.sem.fan, 8)
     sems = [T.sem.aF, T.sem.aS]
     plan = HELP[core % 8]
     for k, d in enumerate(plan):
-        dst = T.cores[_to(rank, d)]
-        rid, pid = topo.addr(dst, core)
-        g.remote_dma(slot, T.ad[:, :], sems[k], T.sem.snt, pid, rid, 0x00FF)
+        rid, pid = topo.addr(T.cores[_to(rank, d)], core)
+        g.remote_dma(_slot(T, d), T.ad[:, :], sems[k], T.sem.snt, pid, rid, 0x00FF)
     g.wait_ge(T.sem.snt, 8 * len(plan))
 
 
 def rank_program(g, core, T, topo):
     rank = T.rank_of(core)
     if rank is None:
-        home = core - core % 8 + RANK_CORE
-        r = T.rank_of(home)
+        r = T.rank_of(core - core % 8 + RANK_CORE)
         if r is not None and core % 8 in HELP:
             _helper(g, core, T, topo, r)
         return
 
-    own = T.ag[:, 256 * rank:256 * rank + 256]
     g.sync.dma_start(T.ad[:, :], T.a[:, :]).then_inc(T.sem.ld_ad, 16)
     g.sync.dma_start(T.ws[:, :], T.w[:, :]).then_inc(T.sem.ld, 16)
-    g.sync.dma_start(own, T.a[:, :]).then_inc(T.sem.ld, 16)
+    g.sync.dma_start(_slot(T, OWN), T.a[:, :]).then_inc(T.sem.ld, 16)
 
     def ids(cs):
         out = []
@@ -66,47 +73,67 @@ def rank_program(g, core, T, topo):
             out.append(DstId(rid=rid, pnc=pid))
         return out
     helpers = [core - RANK_CORE + h for h in FAN_ORDER]
-    direct = [T.cores[_to(rank, d)] for d in DIRECT]
     g.wait_ge(T.sem.ld_ad, 16)
     g.remote_dma_fused([
         RemoteDMATransfer(dst_ids=ids(helpers), dma_engine_mask=0xFF00, remote_sem=T.sem.fan,
                           srcs=[T.ad[:, :]], dsts=[T.ad[:, :] for _ in helpers]),
-        RemoteDMATransfer(dst_ids=ids(direct), dma_engine_mask=0x00FF, remote_sem=T.sem.aR,
-                          srcs=[T.ad[:, :]], dsts=[own for _ in direct]),
+        RemoteDMATransfer(dst_ids=ids([T.cores[_to(rank, d)] for d in D12]), dma_engine_mask=0x00FF,
+                          remote_sem=T.sem.aR, srcs=[T.ad[:, :]], dsts=[_slot(T, d) for d in D12]),
     ], local_sem=T.sem.snt)
+    rid, pid = topo.addr(T.cores[_to(rank, D3)], core)
+    g.remote_dma(_slot(T, D3), T.ad[:, :], T.sem.aD, T.sem.snt, pid, rid, 0x00FF)
+    g.wait_ge(T.sem.aR, 16)
+    rid, pid = topo.addr(T.cores[rank ^ 1], core)
+    g.remote_dma(_slot(T, FWD[0], 2), _slot(T, D12[0], 2), T.sem.aW, T.sem.snt, pid, rid, 0x00FF)
 
-    stages = [
-        (T.sem.ld, 32, [(0, 0, 0)]),
-        (T.sem.aR, 8 * len(DIRECT), DIRECT),
-        (T.sem.aF, 8 * len(HELP), [HELP[h][0] for h in FAN_ORDER]),
-        (T.sem.aS, 8 * sum(1 for h in HELP if len(HELP[h]) > 1), [HELP[h][1] for h in FAN_ORDER if len(HELP[h]) > 1]),
-    ]
-    done = {}
-    pair_order = []
+    stages = [(T.sem.ld, 32, [OWN]), (T.sem.aR, 16, D12), (T.sem.aD, 8, [D3]),
+              (T.sem.aF, 24, WAVE1), (T.sem.aS, 24, WAVE2), (T.sem.aW, 8, FWD)]
+    bank_of = {}
+    for b, ds in enumerate(BANKS):
+        for d in ds:
+            bank_of[d] = b
+    left = [len(ds) for ds in BANKS]
+    bank_order = []
     for sem, val, ds in stages:
         g.tensor.wait_ge(sem, val)
-        js = [_from(rank, d) for d in ds]
-        js.sort(key=lambda j: (0 if done.get(j // 2, 0) else 1, j))
-        for j in js:
-            p = j // 2
+        for d in sorted(ds, key=lambda d: left[bank_of[d]]):
+            b = bank_of[d]
+            j = _from(rank, d)
+            s = SLOTS.index(d)
+            c = 128 * (j % 2) if BANKS[b][0][:2] == BANKS[b][1][:2] else 128 * BANKS[b].index(d)
             for t in range(2):
-                g.tensor.matmul(T["ps%d" % p][:, 128 * (j % 2):128 * (j % 2) + 128],
-                                T.ag[:, 256 * j + 128 * t:256 * j + 128 * t + 128],
+                g.tensor.matmul(T["ps%d" % b][:, c:c + 128],
+                                T.ag[:, 256 * s + 128 * t:256 * s + 128 * t + 128],
                                 T.ws[:, 128 * t:128 * t + 128],
-                                t == 0, t == 1).then_inc(T.sem["mm%d" % p], 1)
-            done[p] = done.get(p, 0) + 1
-            if done[p] == 2:
-                pair_order.append(p)
+                                t == 0, t == 1).then_inc(T.sem["mm%d" % b], 1)
+            left[b] -= 1
+            if left[b] == 0:
+                bank_order.append(b)
 
+    have = {}
     nst = [0, 0]
-    for i, p in enumerate(pair_order):
-        cols = slice(256 * p, 256 * p + 256)
-        g.vector.wait_ge(T.sem["mm%d" % p], 4)
-        g.vector.tensor_copy(T.ys[:, cols], T["ps%d" % p][:, 0:256]).then_inc(T.sem["cp%d" % p], 1)
-        q, st = ((g.sync, T.sem.st_a), (g.scalar, T.sem.st_b))[i % 2]
-        q.wait_ge(T.sem["cp%d" % p], 1)
-        q.dma_start(T.y[:, cols], T.ys[:, cols]).then_inc(st, 16)
-        nst[i % 2] += 16
+    ns = 0
+    for b in bank_order:
+        ds = BANKS[b]
+        g.vector.wait_ge(T.sem["mm%d" % b], 4)
+        if ds[0][:2] == ds[1][:2]:
+            p = _from(rank, ds[0]) // 2
+            g.vector.tensor_copy(T.ys[:, 256 * p:256 * p + 256], T["ps%d" % b][:, 0:256]).then_inc(T.sem["cp%d" % b], 2)
+        else:
+            for i, d in enumerate(ds):
+                j = _from(rank, d)
+                g.vector.tensor_copy(T.ys[:, 128 * j:128 * j + 128],
+                                     T["ps%d" % b][:, 128 * i:128 * i + 128]).then_inc(T.sem["cp%d" % b], 1)
+        for d in ds:
+            p = _from(rank, d) // 2
+            have.setdefault(p, []).append(b)
+            if len(have[p]) == 2:
+                q, st = ((g.sync, T.sem.st_a), (g.scalar, T.sem.st_b))[ns % 2]
+                for bb in sorted(set(have[p])):
+                    q.wait_ge(T.sem["cp%d" % bb], 2)
+                q.dma_start(T.y[:, 256 * p:256 * p + 256], T.ys[:, 256 * p:256 * p + 256]).then_inc(st, 16)
+                nst[ns % 2] += 16
+                ns += 1
     g.sync.wait_ge(T.sem.st_a, nst[0])
     g.scalar.wait_ge(T.sem.st_b, nst[1])
-    g.wait_ge(T.sem.snt, 16)
+    g.wait_ge(T.sem.snt, 32)

from concourse.bass import DstId, RemoteDMATransfer

N = 12
RANK_CORE = 3

OWN = (0, 0, 0)
D12 = [(0, 1, 0), (0, 2, 0)]
D3 = (1, 0, 0)
FWD = [(0, 1, 1), (0, 2, 1)]
HELP = {
    6: [(1, 1, 1), (1, 2, 1)],
    7: [(0, 0, 1), (1, 2, 0)],
    2: [(1, 0, 1), (1, 1, 0)],
}
FAN_ORDER = [6, 7, 2]
WAVE1 = [HELP[h][0] for h in FAN_ORDER]
WAVE2 = [HELP[h][1] for h in FAN_ORDER]
SLOTS = [OWN] + D12 + FWD + [D3] + WAVE1 + WAVE2
BANKS = [D12, [OWN, (0, 0, 1)], [(1, 0, 0), (1, 0, 1)], [(1, 1, 0), (1, 1, 1)], [(1, 2, 0), (1, 2, 1)], FWD]

SCRATCH = {
    "ad": ("dram", [128, 256], "bfloat16"),
    "ag": ("sbuf", [128, N * 256], "bfloat16"),
    "ws": ("sbuf", [128, 256], "bfloat16"),
    "ys": ("sbuf", [128, N * 128], "bfloat16"),
}
for _i in range(len(BANKS)):
    SCRATCH["ps%d" % _i] = ("psum", [128, 512], "float32")

SEMAPHORES = (["ld_ad", "ld", "fan", "snt", "aR", "aD", "aW", "aF", "aS", "st_a", "st_b"]
              + ["mm%d" % i for i in range(len(BANKS))] + ["cp%d" % i for i in range(len(BANKS))])


def _to(r, d):
    return 6 * ((r // 6) ^ d[0]) + 2 * (((r % 6) // 2 + d[1]) % 3) + ((r % 2) ^ d[2])


def _from(r, d):
    return 6 * ((r // 6) ^ d[0]) + 2 * (((r % 6) // 2 - d[1]) % 3) + ((r % 2) ^ d[2])


def _slot(T, d, n=1):
    s = SLOTS.index(d)
    return T.ag[:, 256 * s:256 * (s + n)]


def _helper(g, core, T, topo, rank):
    g.wait_ge(T.sem.fan, 8)
    sems = [T.sem.aF, T.sem.aS]
    plan = HELP[core % 8]
    for k, d in enumerate(plan):
        rid, pid = topo.addr(T.cores[_to(rank, d)], core)
        g.remote_dma(_slot(T, d), T.ad[:, :], sems[k], T.sem.snt, pid, rid, 0x00FF)
    g.wait_ge(T.sem.snt, 8 * len(plan))


def rank_program(g, core, T, topo):
    rank = T.rank_of(core)
    if rank is None:
        r = T.rank_of(core - core % 8 + RANK_CORE)
        if r is not None and core % 8 in HELP:
            _helper(g, core, T, topo, r)
        return

    g.sync.dma_start(T.ad[:, :], T.a[:, :]).then_inc(T.sem.ld_ad, 16)
    g.sync.dma_start(T.ws[:, :], T.w[:, :]).then_inc(T.sem.ld, 16)
    g.sync.dma_start(_slot(T, OWN), T.a[:, :]).then_inc(T.sem.ld, 16)

    def ids(cs):
        out = []
        for c in cs:
            rid, pid = topo.addr(c, core)
            out.append(DstId(rid=rid, pnc=pid))
        return out
    helpers = [core - RANK_CORE + h for h in FAN_ORDER]
    g.wait_ge(T.sem.ld_ad, 16)
    g.remote_dma_fused([
        RemoteDMATransfer(dst_ids=ids(helpers), dma_engine_mask=0xFF00, remote_sem=T.sem.fan,
                          srcs=[T.ad[:, :]], dsts=[T.ad[:, :] for _ in helpers]),
        RemoteDMATransfer(dst_ids=ids([T.cores[_to(rank, d)] for d in D12]), dma_engine_mask=0x00FF,
                          remote_sem=T.sem.aR, srcs=[T.ad[:, :]], dsts=[_slot(T, d) for d in D12]),
    ], local_sem=T.sem.snt)
    rid, pid = topo.addr(T.cores[_to(rank, D3)], core)
    g.remote_dma(_slot(T, D3), T.ad[:, :], T.sem.aD, T.sem.snt, pid, rid, 0x00FF)
    g.wait_ge(T.sem.aR, 16)
    rid, pid = topo.addr(T.cores[rank ^ 1], core)
    g.remote_dma(_slot(T, FWD[0], 2), _slot(T, D12[0], 2), T.sem.aW, T.sem.snt, pid, rid, 0x00FF)

    stages = [(T.sem.ld, 32, [OWN]), (T.sem.aR, 16, D12), (T.sem.aD, 8, [D3]),
              (T.sem.aF, 24, WAVE1), (T.sem.aS, 24, WAVE2), (T.sem.aW, 8, FWD)]
    bank_of = {}
    for b, ds in enumerate(BANKS):
        for d in ds:
            bank_of[d] = b
    left = [len(ds) for ds in BANKS]
    bank_order = []
    for sem, val, ds in stages:
        g.tensor.wait_ge(sem, val)
        for d in sorted(ds, key=lambda d: left[bank_of[d]]):
            b = bank_of[d]
            j = _from(rank, d)
            s = SLOTS.index(d)
            c = 128 * (j % 2) if BANKS[b][0][:2] == BANKS[b][1][:2] else 128 * BANKS[b].index(d)
            for t in range(2):
                g.tensor.matmul(T["ps%d" % b][:, c:c + 128],
                                T.ag[:, 256 * s + 128 * t:256 * s + 128 * t + 128],
                                T.ws[:, 128 * t:128 * t + 128],
                                t == 0, t == 1).then_inc(T.sem["mm%d" % b], 1)
            left[b] -= 1
            if left[b] == 0:
                bank_order.append(b)

    have = {}
    nst = [0, 0]
    ns = 0
    for b in bank_order:
        ds = BANKS[b]
        g.vector.wait_ge(T.sem["mm%d" % b], 4)
        if ds[0][:2] == ds[1][:2]:
            p = _from(rank, ds[0]) // 2
            g.vector.tensor_copy(T.ys[:, 256 * p:256 * p + 256], T["ps%d" % b][:, 0:256]).then_inc(T.sem["cp%d" % b], 2)
        else:
            for i, d in enumerate(ds):
                j = _from(rank, d)
                g.vector.tensor_copy(T.ys[:, 128 * j:128 * j + 128],
                                     T["ps%d" % b][:, 128 * i:128 * i + 128]).then_inc(T.sem["cp%d" % b], 1)
        for d in ds:
            p = _from(rank, d) // 2
            have.setdefault(p, []).append(b)
            if len(have[p]) == 2:
                q, st = ((g.sync, T.sem.st_a), (g.scalar, T.sem.st_b))[ns % 2]
                for bb in sorted(set(have[p])):
                    q.wait_ge(T.sem["cp%d" % bb], 2)
                q.dma_start(T.y[:, 256 * p:256 * p + 256], T.ys[:, 256 * p:256 * p + 256]).then_inc(st, 16)
                nst[ns % 2] += 16
                ns += 1
    g.sync.wait_ge(T.sem.st_a, nst[0])
    g.scalar.wait_ge(T.sem.st_b, nst[1])
    g.wait_ge(T.sem.snt, 32)
